import numpy as np, ml_dtypes
CORES = [3,5,19,21,35,37,51,53,67,69]
N = 10
TK = 256
WID = [32,256,32,160,64,192,32,256,224,96]
def setup_inputs(rng):
    return {"x": rng.standard_normal((N, 128, TK), dtype=np.float32).astype(ml_dtypes.bfloat16), "w1": (rng.standard_normal((N, 128, 128), dtype=np.float32) / 8).astype(ml_dtypes.bfloat16), "w2": (rng.standard_normal((N, 128, 128), dtype=np.float32) / 8).astype(ml_dtypes.bfloat16)}
def setup_inputs_big(rng):
    d = setup_inputs(rng)
    for k in ("x", "w1", "w2"): d[k] = (d[k].astype(np.float32) * 1024.0).astype(d[k].dtype)
    return d
def setup_inputs_small(rng):
    d = setup_inputs(rng)
    for k in ("x", "w1", "w2"): d[k] = (d[k].astype(np.float32) * (1 / 1024.0)).astype(d[k].dtype)
    return d
def setup_inputs_apart(rng):
    d = setup_inputs(rng)
    f = (10.0 ** rng.permutation(np.linspace(-1.5, 1.5, N))).astype(np.float32).reshape(N, 1, 1)
    for k in ("x", "w1", "w2"): d[k] = (d[k].astype(np.float32) * f).astype(d[k].dtype)
    return d
def whole(x, w1, w2):
    X, W1, W2 = x.astype(np.float64), w1.astype(np.float64), w2.astype(np.float64)
    y = np.zeros((N, 128, TK))
    for r in range(N):
        for j in range(N):
            y[r] += W2[j].T @ np.maximum(W1[j].T @ X[r], 0.0)
    return {"y": y.astype(ml_dtypes.bfloat16 if x.dtype != np.float64 else np.float64)}
def reference(x, w1, w2):
    o = whole(x, w1, w2)["y"].copy()
    for r in range(N):
        o[r][:, WID[r]:] = np.nan
    return {"y": o}

from concourse.bass import DstId, RemoteDMATransfer
from concourse.mybir import AluOpType

NR = 10
P = 128
TK = 256
WW = 2 * P
KS = 3
NH = 6
NI = 14

SCRATCH = {
    "wall": ("sbuf", [P, NR * WW], "bfloat16"),
    "xall": ("sbuf", [P, 2 * TK], "bfloat16"),
    "zero": ("sbuf", [P, 2 * TK], "float32"),
    "hs": ("sbuf", [P, NI * 2 * TK], "bfloat16"),
    "psend": ("sbuf", [P, TK], "bfloat16"),
    "pland": ("sbuf", [P, TK], "bfloat16"),
    "ysb": ("sbuf", [P, TK], "bfloat16"),
    "yO": ("psum", [P, 512], "float32"),
    "yP": ("psum", [P, 512], "float32"),
}
for _b in range(NH):
    SCRATCH["hp%d" % _b] = ("psum", [P, 512], "float32")

SEMAPHORES = (["ldw1", "ldw2", "ldx", "xarr", "parr", "sent", "zs", "accO", "accP", "ev", "fin", "stored"]
              + ["arr%d" % _j for _j in range(NR)]
              + ["m1_%d" % _i for _i in range(NI)] + ["rl_%d" % _i for _i in range(NI)])


def _bits(mask):
    return bin(mask).count("1")


def rank_program(g, core, T, topo):
    r = T.rank_of(core)
    if r is None:
        return
    cores = list(T.cores)
    wid = T.tables["WID"]
    S = T.sem
    te, ve, sy, sc = g.tensor, g.vector, g.sync, g.scalar

    chips = []
    for c in cores:
        if topo.chip(c) not in chips:
            chips.append(topo.chip(c))
    nch = len(chips)
    ranks_on = {ch: [q for q in range(len(cores)) if topo.chip(cores[q]) == ch] for ch in chips}
    me = chips.index(topo.chip(core))
    p = [q for q in ranks_on[chips[me]] if q != r][0]

    def split(ch, c):
        same = [q for q in ranks_on[ch] if topo.die(cores[q]) == topo.die(c)]
        other = [q for q in ranks_on[ch] if topo.die(cores[q]) != topo.die(c)]
        return same[0], other[0]

    Wr, Wp = wid[r], wid[p]
    Wc = Wr + Wp

    def slot(j):
        return T.wall[:, j * WW:(j + 1) * WW]

    def dst_id(q):
        rid, pid, _se = topo.addr(cores[q])
        return DstId(rid=rid, pnc=pid)

    far = split(chips[(me + 1) % nch], core)[0]
    m_off = topo.mask(core, cores[far])
    m_on = topo.mask(core, cores[p])
    m_hi = m_on & ~m_off
    m_x = m_hi
    m_p = m_hi if KS < nch - 1 else m_on
    n_off, n_x, n_p = _bits(m_off), _bits(m_x), _bits(m_p)

    sy.dma_start(T.wall[:, r * WW:r * WW + P], T.w1[:, :]).then_inc(S.ldw1, 16)
    sc.dma_start(T.wall[:, r * WW + P:(r + 1) * WW], T.w2[:, :]).then_inc(S.ldw2, 16)
    sy.dma_start(T.xall[:, 0:Wr], T.x[:, 0:Wr]).then_inc(S.ldx, 16)
    ve.memset(T.zero[:, 0:Wc], 0.0).then_inc(S.zs, 1)
    ve.wait_ge(S.zs, 1)

    sent = 0
    g.wait_ge(S.ldw1, 16)
    g.wait_ge(S.ldw2, 16)
    for s in range(1, nch):
        same, other = split(chips[(me + s) % nch], core)
        to = [same] if s <= KS else [same, other]
        for q in to:
            assert topo.may_write(core, cores[q])
        g.remote_dma_fused([RemoteDMATransfer(dst_ids=[dst_id(q) for q in to], dma_engine_mask=m_off,
                                              remote_sem=S["arr%d" % r], srcs=[slot(r)],
                                              dsts=[slot(r) for q in to], alu_op=0)], local_sem=S.sent)
        sent += n_off
        if s == 1:
            rid, pid, _se = topo.addr(cores[p])
            g.wait_ge(S.ldx, 16)
            g.remote_dma(T.xall[:, Wp:Wp + Wr], T.xall[:, 0:Wr], S.xarr, S.sent, pid, rid, m_x)
            sent += n_x

    shared = [r] + [split(chips[(me - s) % nch], core)[0] for s in range(1, KS + 1)]
    items = [(r, 0, Wr), (r, Wr, Wc)]
    for j in shared[1:-1]:
        items.append((j, 0, Wc))
    if len(shared) > 1:
        items += [(shared[-1], Wr, Wc), (shared[-1], 0, Wr)]
    for s in range(KS + 1, nch):
        for j in split(chips[(me - s) % nch], core):
            items.append((j, 0, Wr))
    n = len(items)
    assert n <= NI
    i_ev = max(i for i in range(n) if items[i][2] > Wr)
    n_o = sum(1 for it in items if it[1] < Wr)
    n_p_parts = sum(1 for it in items if it[2] > Wr)

    waited = {}

    def need(q, name, sem, val):
        if waited.get((name, sem), 0) < val:
            q.wait_ge(S[sem], val)
            waited[(name, sem)] = val

    cnt = {"O": 0, "P": 0}

    def mm1(i):
        j, lo, hi = items[i]
        if j == r:
            need(te, "t", "ldw1", 16)
        else:
            need(te, "t", "arr%d" % j, n_off)
        if lo < Wr:
            need(te, "t", "ldx", 16)
        if hi > Wr:
            need(te, "t", "xarr", n_x)
        if i >= NH:
            need(te, "t", "rl_%d" % (i - NH), 1)
        te.matmul(T["hp%d" % (i % NH)][:, 0:hi - lo], T.wall[:, j * WW:j * WW + P], T.xall[:, lo:hi],
                  start=True, stop=True).then_inc(S["m1_%d" % i], 1)

    def mm2(i):
        j, lo, hi = items[i]
        need(te, "t", "rl_%d" % i, 1)
        if j == r:
            need(te, "t", "ldw2", 16)
        w2 = T.wall[:, j * WW + P:(j + 1) * WW]
        b = i * 2 * TK
        if hi > Wr:
            a = max(lo, Wr)
            te.matmul(T.yP[:, a - Wr:hi - Wr], w2, T.hs[:, b + a - lo:b + hi - lo],
                      start=(cnt["P"] == 0), stop=(cnt["P"] == n_p_parts - 1)).then_inc(S.accP, 1)
            cnt["P"] += 1
        if lo < Wr:
            e = min(hi, Wr)
            te.matmul(T.yO[:, lo:e], w2, T.hs[:, b:b + e - lo],
                      start=(cnt["O"] == 0), stop=(cnt["O"] == n_o - 1)).then_inc(S.accO, 1)
            cnt["O"] += 1

    pend = None
    for i in range(n):
        if pend is not None and pend == i_ev and items[i][0] != items[pend][0]:
            mm2(pend)
            pend = None
        mm1(i)
        if pend is not None:
            mm2(pend)
        pend = i
    mm2(pend)

    for i in range(n):
        j, lo, hi = items[i]
        ve.wait_ge(S["m1_%d" % i], 1)
        ve.tensor_tensor(T.hs[:, i * 2 * TK:i * 2 * TK + hi - lo], T["hp%d" % (i % NH)][:, 0:hi - lo],
                         T.zero[:, 0:hi - lo], AluOpType.max).then_inc(S["rl_%d" % i], 1)
        if i == i_ev:
            ve.wait_ge(S.accP, n_p_parts)
            ve.tensor_copy(T.psend[:, 0:Wp], T.yP[:, 0:Wp]).then_inc(S.ev, 1)
    ve.wait_ge(S.accO, n_o)
    ve.wait_ge(S.parr, n_p)
    ve.tensor_tensor(T.ysb[:, 0:Wr], T.yO[:, 0:Wr], T.pland[:, 0:Wr], AluOpType.add).then_inc(S.fin, 1)

    rid, pid, _se = topo.addr(cores[p])
    g.wait_ge(S.ev, 1)
    g.remote_dma(T.pland[:, 0:Wp], T.psend[:, 0:Wp], S.parr, S.sent, pid, rid, m_p)
    sent += n_p
    g.wait_ge(S.sent, sent)

    sy.wait_ge(S.fin, 1)
    sy.dma_start(T.y[:, 0:Wr], T.ysb[:, 0:Wr]).then_inc(S.stored, 16)
    sy.wait_ge(S.stored, 16)
